import numpy as np
import ml_dtypes


def mxq(x, axis, fmt="e4m3"):
    dtype, down = {"e4m3": (ml_dtypes.float8_e4m3fn, 7), "e5m2": (ml_dtypes.float8_e5m2, 14)}[fmt]
    v = np.moveaxis(np.asarray(x, np.float32).astype(ml_dtypes.bfloat16).astype(np.float64), axis, -1)
    blocks = v.reshape(v.shape[:-1] + (-1, 32))
    amax = np.abs(blocks).max(-1, keepdims=True)
    byte = np.maximum(np.where(amax > 0, np.frexp(amax)[1] - 1 + 127, 0) - down, 1)
    scale = np.exp2(byte - 127.0)
    codes = (blocks / scale).astype(np.float32).astype(dtype).astype(np.float64)
    return np.moveaxis((codes * scale).reshape(v.shape), -1, axis)


WIDE = False


def mx_kscale(k):
    if not WIDE:
        return np.ones(k)
    levels = np.array([10, -10, 5, -5, 0])
    if k % 512:
        return np.exp2(np.random.permutation(np.resize(levels, k // 32))).repeat(32)
    a = np.empty((k // 512, 16))
    for p in range(k // 512):
        a[p, :8] = np.random.permutation(np.resize(levels, 8))
        for g in range(8):
            far = levels[np.abs(levels - a[p, g]) >= 10]
            a[p, g + 8] = far[np.random.randint(len(far))]
    return np.exp2(a.ravel()).repeat(32)


def f64(x):
    return np.asarray(x).astype(np.float64)


def striped(idx):
    return np.tile(idx.reshape(-1, 16).T, (8, 1)).astype(np.uint16)


def unstriped(offs):
    return offs[:16].T.reshape(-1).astype(np.int64)


E2M1 = np.array([0.0, 0.5, 1.0, 1.5, 2.0, 3.0, 4.0, 6.0, -0.0, -0.5, -1.0, -1.5, -2.0, -3.0, -4.0, -6.0])


def pack_weight(w, fmt):
    k, n = w.shape
    w = f64(np.asarray(w, np.float32).astype(ml_dtypes.bfloat16)).reshape(k // 32, 32, n)
    amax = np.abs(w).max(1)
    if fmt == "e4m3":
        byte = np.frexp(amax)[1] - 1 + 127 - 7
    else:
        mant, ex = np.frexp(amax / 6.0)
        byte = np.where(mant > 0.5, ex, ex - 1) + 127
    byte = np.clip(np.where(amax > 0, byte, 1), 1, 254)
    scaled = (w * np.exp2(127.0 - byte)[:, None, :]).reshape(k, n).astype(np.float32)
    by_word = np.ascontiguousarray(scaled.reshape(k // 512, 128, 4, n).transpose(0, 1, 3, 2))
    if fmt == "e4m3":
        words = by_word.astype(ml_dtypes.float8_e4m3fn).view(np.uint8)
    else:
        c = by_word.astype(ml_dtypes.float4_e2m1fn).view(np.uint8) & 0xF
        words = (c[..., 0::2] | (c[..., 1::2] << 4)).reshape(k // 512, 128, 2 * n)
    return np.ascontiguousarray(words), np.ascontiguousarray(byte.astype(np.uint8).reshape(k // 512, 16, n))


def unpack_weight(words, scales, fmt):
    g, _, n = scales.shape
    words = np.ascontiguousarray(words).reshape(g, 128, n, -1)
    if fmt == "e4m3":
        vals = words.view(ml_dtypes.float8_e4m3fn).astype(np.float64)
    else:
        nib = np.empty((g, 128, n, 4), np.uint8)
        nib[..., 0::2] = words & 0xF
        nib[..., 1::2] = words >> 4
        vals = E2M1[nib]
    vals = vals * np.repeat(np.exp2(scales.astype(np.float64) - 127.0), 8, axis=1)[..., None]
    return vals.transpose(0, 1, 3, 2).reshape(g * 512, n)


def gelu(v):
    return 0.5 * v * (1.0 + np.tanh(np.sqrt(2.0 / np.pi) * (v + 0.044715 * v**3)))


K, H, T, S, T2 = 1024, 512, 4096, 1024, 2048


def setup_inputs():
    n = np.random.standard_normal
    s = mx_kscale(K)[:, None]
    u = mx_kscale(H)[:, None]
    tab_words, tab_scales = pack_weight(n((K, T)) * s, "e4m3")
    wb_words, wb_scales = pack_weight(0.8 * n((K, H)) / np.sqrt(K) / s * u.T, "e2m1")
    wc_words, wc_scales = pack_weight(0.8 * n((H, H)) / np.sqrt(H) / u, "e4m3")
    return {
        "tab_words": tab_words, "tab_scales": tab_scales,
        "offs": striped(np.random.permutation(T)[:S]),
        "offs2": striped(np.random.permutation(T)[:S]),
        "offs3": striped(np.random.permutation(T2)[:S]),
        "wa": (0.8 * n((K, H)) / np.sqrt(K) / s * u.T).astype(np.float32),
        "wb_words": wb_words, "wb_scales": wb_scales,
        "wg": (1.2 * n((K, H)) / np.sqrt(K) / s * u.T).astype(np.float32),
        "wc_words": wc_words, "wc_scales": wc_scales,
        "d": (0.7 * n(H) / u[:, 0]).astype(np.float32),
        "wgo": np.exp(0.3 * n((128, S))).astype(np.float32),
    }


def reference(tab_words, tab_scales, offs, offs2, offs3, wa, wb_words, wb_scales,
              wg, wc_words, wc_scales, d, wgo):
    TW = unpack_weight(tab_words, tab_scales, "e4m3")
    v = TW[:, unstriped(offs)]
    v2 = TW[:, unstriped(offs2)]
    wb = unpack_weight(wb_words, wb_scales, "e2m1")
    wc = unpack_weight(wc_words, wc_scales, "e4m3")
    both = np.abs(mxq(f64(wa), 0, "e4m3").T @ v + wb.T @ v2)
    x = np.maximum(both, mxq(f64(wg), 0, "e4m3").T @ v)
    mixed = wc.T @ mxq(x, 0, "e4m3")
    y = np.tanh(mixed + f64(d)[:, None] * x)
    out = np.zeros((H, T2))
    out[:, unstriped(offs3)] = np.tile(f64(wgo), (H // 128, 1)) * y
    return out

@@ -1,0 +1,270 @@
+from contextlib import ExitStack
+
+import concourse.mybir as mybir
+
+K, H, T, S, T2 = 1024, 512, 4096, 1024, 2048
+FLOPS = 2 * S * H * (3 * K + H)
+
+F32 = mybir.dt.float32
+BF16 = mybir.dt.bfloat16
+I32 = mybir.dt.int32
+U32 = mybir.dt.uint32
+U16 = mybir.dt.uint16
+U8 = mybir.dt.uint8
+FP8X4 = mybir.dt.float8_e4m3fn_x4
+FP4X4 = mybir.dt.float4_e2m1fn_x4
+ACT = mybir.ActivationFunctionType
+ALU = mybir.AluOpType
+
+P = 128
+PACK = 4
+PASSES = K // (P * PACK)
+CHUNK = 256
+CHUNKS = S // CHUNK
+HALF = 512
+LANES = 16
+
+
+def tile_list_laser_link_slots_kernel(
+    tc, tab_words, tab_scales, offs, offs2, offs3, wa, wb_words, wb_scales, wg, wc_words, wc_scales, d, wgo, out
+):
+    nc = tc.nc
+    with ExitStack() as ctx:
+        keep = ctx.enter_context(tc.tile_pool(name="keep", bufs=1))
+        ring = ctx.enter_context(tc.tile_pool(name="ring", bufs=2))
+        psum = ctx.enter_context(tc.psum_pool(name="psum", bufs=1))
+
+        lists = [keep.tile([P, S // LANES], U16, name=f"list{i}") for i in range(3)]
+        tab_sc = keep.tile([P, T], U8, name="tab_sc", align_bytes=64)
+        w_sc_raw = keep.tile([P, PASSES + 1, H], U8, name="w_sc_raw", align_bytes=64)
+        rx_sc_last = keep.tile([P, S], U8, name="rx_sc_last", align_bytes=64)
+        nc.gpsimd.memset(tab_sc[:].bitcast(I32), 0)
+        nc.gpsimd.memset(w_sc_raw[:].rearrange("p a c -> p (a c)").bitcast(I32), 0)
+        nc.gpsimd.memset(rx_sc_last[:].bitcast(I32), 0)
+
+        nc.sync.dma_start(lists[0][:], offs)
+        nc.sync.dma_start(lists[1][:], offs2)
+
+        def load_weight(w, a, name):
+            rows = w[a * HALF : (a + 1) * HALF, :].rearrange("(p j) c -> p j c", j=PACK)
+            halves = []
+            for h in range(2):
+                raw = keep.tile([P, PACK, H // 2], F32, name=f"{name}_{h}")
+                nc.sync.dma_start(out=raw[:], in_=rows[:, :, h * H // 2 : (h + 1) * H // 2])
+                halves.append(raw)
+            return halves
+
+        def load_table(a):
+            words = keep.tile([P, T], U32, name=f"tab{a}", align_bytes=64)
+            nc.sync.dma_start(out=words[:].bitcast(I32), in_=tab_words[a].rearrange("p t i -> p (t i)").bitcast(I32))
+            return words
+
+        wb_raw = keep.tile([P, PASSES, 2 * H], U8, name="wb_raw", align_bytes=64)
+        nc.sync.dma_start(out=wb_raw[:].bitcast(I32), in_=wb_words.rearrange("a p b -> p a b").bitcast(I32))
+        wa_raw0 = load_weight(wa, 0, "wa_raw0")
+        for q in range(4):
+            nc.sync.dma_start(
+                out=tab_sc[32 * q : 32 * q + 4 * PASSES, :].bitcast(I32),
+                in_=tab_scales[:, 4 * q : 4 * q + 4, :].bitcast(I32),
+            )
+        tab0 = load_table(0)
+        for q in range(4):
+            nc.sync.dma_start(
+                out=w_sc_raw[32 * q : 32 * q + 4, 0:PASSES, :].bitcast(I32),
+                in_=wb_scales[:, 4 * q : 4 * q + 4, :].rearrange("a r c -> r a c").bitcast(I32),
+            )
+        wg_raw0 = load_weight(wg, 0, "wg_raw0")
+        wc_raw = keep.tile([P, H], U32, name="wc_raw", align_bytes=64)
+        nc.sync.dma_start(out=wc_raw[:].bitcast(I32), in_=wc_words[0].rearrange("p c i -> p (c i)").bitcast(I32))
+        tab1 = load_table(1)
+        for q in range(4):
+            nc.sync.dma_start(
+                out=w_sc_raw[32 * q : 32 * q + 4, PASSES, :].bitcast(I32),
+                in_=wc_scales[0, 4 * q : 4 * q + 4, :].bitcast(I32),
+            )
+        wa_raw1 = load_weight(wa, 1, "wa_raw1")
+        wg_raw1 = load_weight(wg, 1, "wg_raw1")
+        nc.sync.dma_start(lists[2][:], offs3)
+        d_sb = keep.tile([P, PACK], F32, name="d_sb")
+        nc.sync.dma_start(out=d_sb[:], in_=d.rearrange("(p t) -> p t", t=PACK))
+        wgo_rows = wgo.rearrange("(m t) s -> t m s", t=PACK)
+        wgo_sb = [keep.tile([P, S], F32, name=f"wgo{t}") for t in range(PACK)]
+        for t in range(PACK):
+            nc.sync.dma_start(out=wgo_sb[t][:], in_=wgo_rows[t].unsqueeze(0).to_broadcast([4, 32, S]))
+
+        wb_w = keep.tile([P, PASSES, PACK, P], U16, name="wb_w", align_bytes=64)
+        nc.vector.tensor_copy(out=wb_w[:], in_=wb_raw[:].bitcast(U16).rearrange("p a (m t) -> p a t m", t=PACK))
+
+        tx_sc = keep.tile([P, S], U8, name="tx_sc", align_bytes=64)
+        rx_sc = keep.tile([P, S], U8, name="rx_sc", align_bytes=64)
+        nc.vector.tensor_copy(rx_sc[:], tab_sc[:].indirect(lists[1][:]))
+        nc.vector.tensor_copy(tx_sc[:], tab_sc[:].indirect(lists[0][:]))
+        for q in range(4):
+            nc.gpsimd.dma_start(
+                out=rx_sc_last[32 * q : 32 * q + 4, :].bitcast(I32),
+                in_=rx_sc[32 * q + 4 : 32 * q + 8, :].bitcast(I32),
+            )
+        pages = [keep.tile([P, T2], F32, name=f"page{t}") for t in range(PACK)]
+        for t in range(PACK):
+            nc.gpsimd.memset(pages[t][:], 0.0)
+
+        w_sc = keep.tile([P, PASSES + 1, PACK, P], U8, name="w_sc", align_bytes=64)
+        dealt = w_sc_raw[:].rearrange("p a (m t) -> p a t m", t=PACK)
+        nc.gpsimd.tensor_copy(out=w_sc[:, 0:PASSES], in_=dealt[:, 0:PASSES])
+        wc_w = keep.tile([P, PACK, P], U32, name="wc_w", align_bytes=64)
+        nc.gpsimd.tensor_copy(
+            out=wc_w[:].rearrange("p t (c i) -> p c t i", i=4),
+            in_=wc_raw[:].rearrange("p (c i t) -> p c t i", i=4, t=PACK),
+        )
+        nc.gpsimd.tensor_copy(out=w_sc[:, PASSES], in_=dealt[:, PASSES])
+
+        def quantize_weight(halves, name, share_with_vector=False):
+            grouped = ring.tile([P, PACK, P, PACK], BF16, name="grouped", align_bytes=64)
+            for h, raw in enumerate(halves):
+                dst = grouped[:, :, h * P // 2 : (h + 1) * P // 2, :].rearrange("p t m j -> p m t j")
+                src = raw[:].rearrange("p j (m t) -> p m t j", t=PACK)
+                if share_with_vector and h == 1:
+                    nc.vector.tensor_copy(out=dst, in_=src)
+                else:
+                    nc.scalar.activation(out=dst, in_=src, func=ACT.Copy)
+            codes = keep.tile([P, H], U32, name=name + "_codes", align_bytes=64)
+            plane = keep.tile([P, H], U8, name=name + "_plane", align_bytes=64)
+            nc.vector.quantize_mx(
+                out=codes[:].bitcast(FP8X4), scales=plane[:], in_=grouped[:].rearrange("p t m j -> p (t m j)")
+            )
+            return codes, plane
+
+        def gather_words(words, a):
+            picked = {}
+            for h in range(S // HALF):
+                for i in range(2):
+                    g = keep.tile([P, HALF], U32, name=f"picked{a}{h}{i}", align_bytes=64)
+                    cols = slice(h * HALF // LANES, (h + 1) * HALF // LANES)
+                    nc.vector.tensor_copy(g[:], words[:].indirect(lists[i][:, cols]))
+                    picked[i, h] = g
+            return picked
+
+        wa_q = [quantize_weight(wa_raw0, "wa0")]
+        picked0 = gather_words(tab0, 0)
+        wg_q = [quantize_weight(wg_raw0, "wg0")]
+        picked1 = gather_words(tab1, 1)
+        wa_q.append(quantize_weight(wa_raw1, "wa1"))
+        wg_q.append(quantize_weight(wg_raw1, "wg1", share_with_vector=True))
+        picked = [picked0, picked1]
+
+        banks = [psum.tile([P, 2, CHUNK], F32, name=f"bank{b}") for b in range(8)]
+        pair_a = [0, 2, 1, 0]
+        pair_g = [1, 3, 2, 1]
+        pair_m = [0, 3, 2, 3]
+        y = keep.tile([P, PACK, S], F32, name="y")
+
+        def moving(i, a, c):
+            h, o = divmod(c * CHUNK, HALF)
+            return picked[a][i, h][:, o : o + CHUNK].bitcast(FP8X4)
+
+        def stage1(c):
+            cols = slice(c * CHUNK, (c + 1) * CHUNK)
+            x = ring.tile([P, PACK, CHUNK], F32, name="x", bufs=3)
+            size = ring.tile([P, PACK, CHUNK], F32, name="size")
+            for b in range(2):
+                bank = banks[2 * pair_a[c] + b]
+                for a in range(PASSES):
+                    for u in range(2):
+                        t = 2 * b + u
+                        m = slice(t * P, (t + 1) * P)
+                        nc.tensor.matmul_mx(
+                            out=bank[:, u, :],
+                            lhsT=wa_q[a][0][:, m].bitcast(FP8X4),
+                            lhsT_scale=wa_q[a][1][:, m],
+                            rhs=moving(0, a, c),
+                            rhs_scale=tx_sc[4 * a : P, cols],
+                            start=(a == 0 and u == 0),
+                            stop=False,
+                        )
+                        nc.tensor.matmul_mx(
+                            out=bank[:, u, :],
+                            lhsT=wb_w[:, a, t, :].bitcast(FP4X4),
+                            lhsT_scale=w_sc[:, a, t, :],
+                            rhs=moving(1, a, c),
+                            rhs_scale=(rx_sc if a == 0 else rx_sc_last)[:, cols],
+                            start=False,
+                            stop=(a == PASSES - 1 and u == 1),
+                        )
+                nc.scalar.activation(out=size[:, 2 * b : 2 * b + 2, :], in_=bank[:], func=ACT.Abs)
+            for b in range(2):
+                bank = banks[2 * pair_g[c] + b]
+                for a in range(PASSES):
+                    for u in range(2):
+                        t = 2 * b + u
+                        m = slice(t * P, (t + 1) * P)
+                        nc.tensor.matmul_mx(
+                            out=bank[:, u, :],
+                            lhsT=wg_q[a][0][:, m].bitcast(FP8X4),
+                            lhsT_scale=wg_q[a][1][:, m],
+                            rhs=moving(0, a, c),
+                            rhs_scale=tx_sc[4 * a : P, cols],
+                            start=(a == 0 and u == 0),
+                            stop=(a == PASSES - 1 and u == 1),
+                        )
+                nc.vector.tensor_tensor(
+                    out=x[:, 2 * b : 2 * b + 2, :], in0=bank[:], in1=size[:, 2 * b : 2 * b + 2, :], op=ALU.max
+                )
+            x_bf = ring.tile([P, CHUNK, PACK], BF16, name="x_bf", align_bytes=64)
+            nc.scalar.copy(
+                out=x_bf[:].rearrange("p (c i) t -> p c t i", i=4),
+                in_=x[:].rearrange("p t (c i) -> p c t i", i=4),
+            )
+            codes = ring.tile([P, CHUNK], U32, name="x_codes", align_bytes=64)
+            plane = ring.tile([P, CHUNK], U8, name="x_plane", align_bytes=64)
+            nc.vector.quantize_mx(
+                out=codes[:].bitcast(FP8X4), scales=plane[:], in_=x_bf[:].rearrange("p c t -> p (c t)")
+            )
+            return x, codes, plane
+
+        def stage2(c, x, codes, plane):
+            cols = slice(c * CHUNK, (c + 1) * CHUNK)
+            for b in range(2):
+                bank = banks[2 * pair_m[c] + b]
+                for u in range(2):
+                    t = 2 * b + u
+                    nc.tensor.matmul_mx(
+                        out=bank[:, u, :],
+                        lhsT=wc_w[:, t, :].bitcast(FP8X4),
+                        lhsT_scale=w_sc[:, PASSES, t, :],
+                        rhs=codes[:].bitcast(FP8X4),
+                        rhs_scale=plane[:],
+                        start=True,
+                        stop=True,
+                    )
+                z = ring.tile([P, 2, CHUNK], F32, name="z", bufs=3)
+                for u in range(2):
+                    t = 2 * b + u
+                    nc.vector.scalar_tensor_tensor(
+                        out=z[:, u, :], in0=x[:, t, :], scalar=d_sb[:, t : t + 1], in1=bank[:, u, :],
+                        op0=ALU.mult, op1=ALU.add,
+                    )
+                nc.scalar.activation(out=y[:, 2 * b : 2 * b + 2, cols], in_=z[:], func=ACT.Tanh)
+
+        def scatter(t, lo, hi):
+            nc.vector.tensor_tensor(
+                pages[t][:].indirect(lists[2][:, lo // LANES : hi // LANES]),
+                y[:, t, lo:hi],
+                wgo_sb[t][:, lo:hi],
+                ALU.mult,
+            )
+
+        made0 = stage1(0)
+        made1 = stage1(1)
+        stage2(0, *made0)
+        stage2(1, *made1)
+        made2 = stage1(2)
+        made3 = stage1(3)
+        stage2(2, *made2)
+        stage2(3, *made3)
+        out_rows = out.rearrange("(p t) s -> t p s", t=PACK)
+        for c in range(2):
+            for t in range(PACK):
+                scatter(t, c * CHUNK, (c + 1) * CHUNK)
+        for t in range(PACK):
+            scatter(t, HALF, S)
+            nc.sync.dma_start(out=out_rows[t], in_=pages[t][:])

@@ -38,9 +38,9 @@ def tile_list_laser_link_slots_kernel(
         tab_sc = keep.tile([P, T], U8, name="tab_sc", align_bytes=64)
         w_sc_raw = keep.tile([P, PASSES + 1, H], U8, name="w_sc_raw", align_bytes=64)
         rx_sc_last = keep.tile([P, S], U8, name="rx_sc_last", align_bytes=64)
-        nc.gpsimd.memset(tab_sc[:].bitcast(I32), 0)
-        nc.gpsimd.memset(w_sc_raw[:].rearrange("p a c -> p (a c)").bitcast(I32), 0)
-        nc.gpsimd.memset(rx_sc_last[:].bitcast(I32), 0)
+        nc.vector.memset(tab_sc[:].bitcast(I32), 0)
+        nc.vector.memset(w_sc_raw[:].rearrange("p a c -> p (a c)").bitcast(I32), 0)
+        nc.vector.memset(rx_sc_last[:].bitcast(I32), 0)
 
         nc.sync.dma_start(lists[0][:], offs)
         nc.sync.dma_start(lists[1][:], offs2)
@@ -59,8 +59,6 @@ def tile_list_laser_link_slots_kernel(
             nc.sync.dma_start(out=words[:].bitcast(I32), in_=tab_words[a].rearrange("p t i -> p (t i)").bitcast(I32))
             return words
 
-        wb_raw = keep.tile([P, PASSES, 2 * H], U8, name="wb_raw", align_bytes=64)
-        nc.sync.dma_start(out=wb_raw[:].bitcast(I32), in_=wb_words.rearrange("a p b -> p a b").bitcast(I32))
         wa_raw0 = load_weight(wa, 0, "wa_raw0")
         for q in range(4):
             nc.sync.dma_start(
@@ -68,22 +66,24 @@ def tile_list_laser_link_slots_kernel(
                 in_=tab_scales[:, 4 * q : 4 * q + 4, :].bitcast(I32),
             )
         tab0 = load_table(0)
+        wb_raw = keep.tile([P, PASSES, 2 * H], U8, name="wb_raw", align_bytes=64)
+        nc.sync.dma_start(out=wb_raw[:].bitcast(I32), in_=wb_words.rearrange("a p b -> p a b").bitcast(I32))
         for q in range(4):
             nc.sync.dma_start(
                 out=w_sc_raw[32 * q : 32 * q + 4, 0:PASSES, :].bitcast(I32),
                 in_=wb_scales[:, 4 * q : 4 * q + 4, :].rearrange("a r c -> r a c").bitcast(I32),
             )
         wg_raw0 = load_weight(wg, 0, "wg_raw0")
+        tab1 = load_table(1)
+        wa_raw1 = load_weight(wa, 1, "wa_raw1")
+        wg_raw1 = load_weight(wg, 1, "wg_raw1")
         wc_raw = keep.tile([P, H], U32, name="wc_raw", align_bytes=64)
         nc.sync.dma_start(out=wc_raw[:].bitcast(I32), in_=wc_words[0].rearrange("p c i -> p (c i)").bitcast(I32))
-        tab1 = load_table(1)
         for q in range(4):
             nc.sync.dma_start(
                 out=w_sc_raw[32 * q : 32 * q + 4, PASSES, :].bitcast(I32),
                 in_=wc_scales[0, 4 * q : 4 * q + 4, :].bitcast(I32),
             )
-        wa_raw1 = load_weight(wa, 1, "wa_raw1")
-        wg_raw1 = load_weight(wg, 1, "wg_raw1")
         nc.sync.dma_start(lists[2][:], offs3)
         d_sb = keep.tile([P, PACK], F32, name="d_sb")
         nc.sync.dma_start(out=d_sb[:], in_=d.rearrange("(p t) -> p t", t=PACK))
@@ -92,8 +92,17 @@ def tile_list_laser_link_slots_kernel(
         for t in range(PACK):
             nc.sync.dma_start(out=wgo_sb[t][:], in_=wgo_rows[t].unsqueeze(0).to_broadcast([4, 32, S]))
 
+        pages = [keep.tile([P, T2], F32, name=f"page{t}") for t in range(PACK)]
+        for t in range(PACK):
+            nc.vector.memset(pages[t][:].bitcast(I32), 0)
+
         wb_w = keep.tile([P, PASSES, PACK, P], U16, name="wb_w", align_bytes=64)
         nc.vector.tensor_copy(out=wb_w[:], in_=wb_raw[:].bitcast(U16).rearrange("p a (m t) -> p a t m", t=PACK))
+        wc_w = keep.tile([P, PACK, P], U32, name="wc_w", align_bytes=64)
+        nc.vector.tensor_copy(
+            out=wc_w[:].rearrange("p t (c i) -> p c t i", i=4),
+            in_=wc_raw[:].rearrange("p (c i t) -> p c t i", i=4, t=PACK),
+        )
 
         tx_sc = keep.tile([P, S], U8, name="tx_sc", align_bytes=64)
         rx_sc = keep.tile([P, S], U8, name="rx_sc", align_bytes=64)
@@ -104,29 +113,17 @@ def tile_list_laser_link_slots_kernel(
                 out=rx_sc_last[32 * q : 32 * q + 4, :].bitcast(I32),
                 in_=rx_sc[32 * q + 4 : 32 * q + 8, :].bitcast(I32),
             )
-        pages = [keep.tile([P, T2], F32, name=f"page{t}") for t in range(PACK)]
-        for t in range(PACK):
-            nc.gpsimd.memset(pages[t][:], 0.0)
-
         w_sc = keep.tile([P, PASSES + 1, PACK, P], U8, name="w_sc", align_bytes=64)
         dealt = w_sc_raw[:].rearrange("p a (m t) -> p a t m", t=PACK)
-        nc.gpsimd.tensor_copy(out=w_sc[:, 0:PASSES], in_=dealt[:, 0:PASSES])
-        wc_w = keep.tile([P, PACK, P], U32, name="wc_w", align_bytes=64)
-        nc.gpsimd.tensor_copy(
-            out=wc_w[:].rearrange("p t (c i) -> p c t i", i=4),
-            in_=wc_raw[:].rearrange("p (c i t) -> p c t i", i=4, t=PACK),
-        )
-        nc.gpsimd.tensor_copy(out=w_sc[:, PASSES], in_=dealt[:, PASSES])
+        nc.vector.tensor_copy(out=w_sc[:, 0:PASSES], in_=dealt[:, 0:PASSES])
+        nc.vector.tensor_copy(out=w_sc[:, PASSES], in_=dealt[:, PASSES])
 
-        def quantize_weight(halves, name, share_with_vector=False):
+        def quantize_weight(halves, name):
             grouped = ring.tile([P, PACK, P, PACK], BF16, name="grouped", align_bytes=64)
             for h, raw in enumerate(halves):
                 dst = grouped[:, :, h * P // 2 : (h + 1) * P // 2, :].rearrange("p t m j -> p m t j")
                 src = raw[:].rearrange("p j (m t) -> p m t j", t=PACK)
-                if share_with_vector and h == 1:
-                    nc.vector.tensor_copy(out=dst, in_=src)
-                else:
-                    nc.scalar.activation(out=dst, in_=src, func=ACT.Copy)
+                nc.scalar.activation(out=dst, in_=src, func=ACT.Copy)
             codes = keep.tile([P, H], U32, name=name + "_codes", align_bytes=64)
             plane = keep.tile([P, H], U8, name=name + "_plane", align_bytes=64)
             nc.vector.quantize_mx(
@@ -149,7 +146,7 @@ def tile_list_laser_link_slots_kernel(
         wg_q = [quantize_weight(wg_raw0, "wg0")]
         picked1 = gather_words(tab1, 1)
         wa_q.append(quantize_weight(wa_raw1, "wa1"))
-        wg_q.append(quantize_weight(wg_raw1, "wg1", share_with_vector=True))
+        wg_q.append(quantize_weight(wg_raw1, "wg1"))
         picked = [picked0, picked1]
 
         banks = [psum.tile([P, 2, CHUNK], F32, name=f"bank{b}") for b in range(8)]

@@ -38,7 +38,8 @@ def tile_list_laser_link_slots_kernel(
         tab_sc = keep.tile([P, T], U8, name="tab_sc", align_bytes=64)
         w_sc_raw = keep.tile([P, PASSES + 1, H], U8, name="w_sc_raw", align_bytes=64)
         rx_sc_last = keep.tile([P, S], U8, name="rx_sc_last", align_bytes=64)
-        nc.vector.memset(tab_sc[:].bitcast(I32), 0)
+        nc.gpsimd.memset(tab_sc[:, : T // 2].bitcast(I32), 0)
+        nc.vector.memset(tab_sc[:, T // 2 :].bitcast(I32), 0)
         nc.vector.memset(w_sc_raw[:].rearrange("p a c -> p (a c)").bitcast(I32), 0)
         nc.vector.memset(rx_sc_last[:].bitcast(I32), 0)
 
@@ -59,41 +60,42 @@ def tile_list_laser_link_slots_kernel(
             nc.sync.dma_start(out=words[:].bitcast(I32), in_=tab_words[a].rearrange("p t i -> p (t i)").bitcast(I32))
             return words
 
-        wa_raw0 = load_weight(wa, 0, "wa_raw0")
+        wb_raw = keep.tile([P, PASSES, 2 * H], U8, name="wb_raw", tag="early2", align_bytes=64)
+        nc.sync.dma_start(out=wb_raw[:].bitcast(I32), in_=wb_words.rearrange("a p b -> p a b").bitcast(I32))
+        wc_raw = keep.tile([P, H], U32, name="wc_raw", tag="early3", align_bytes=64)
+        nc.sync.dma_start(out=wc_raw[:].bitcast(I32), in_=wc_words[0].rearrange("p c i -> p (c i)").bitcast(I32))
         for q in range(4):
             nc.sync.dma_start(
                 out=tab_sc[32 * q : 32 * q + 4 * PASSES, :].bitcast(I32),
                 in_=tab_scales[:, 4 * q : 4 * q + 4, :].bitcast(I32),
             )
         tab0 = load_table(0)
-        wb_raw = keep.tile([P, PASSES, 2 * H], U8, name="wb_raw", align_bytes=64)
-        nc.sync.dma_start(out=wb_raw[:].bitcast(I32), in_=wb_words.rearrange("a p b -> p a b").bitcast(I32))
         for q in range(4):
             nc.sync.dma_start(
                 out=w_sc_raw[32 * q : 32 * q + 4, 0:PASSES, :].bitcast(I32),
                 in_=wb_scales[:, 4 * q : 4 * q + 4, :].rearrange("a r c -> r a c").bitcast(I32),
             )
-        wg_raw0 = load_weight(wg, 0, "wg_raw0")
-        tab1 = load_table(1)
-        wa_raw1 = load_weight(wa, 1, "wa_raw1")
-        wg_raw1 = load_weight(wg, 1, "wg_raw1")
-        wc_raw = keep.tile([P, H], U32, name="wc_raw", align_bytes=64)
-        nc.sync.dma_start(out=wc_raw[:].bitcast(I32), in_=wc_words[0].rearrange("p c i -> p (c i)").bitcast(I32))
+        wa_raw0 = load_weight(wa, 0, "wa_raw0")
         for q in range(4):
             nc.sync.dma_start(
                 out=w_sc_raw[32 * q : 32 * q + 4, PASSES, :].bitcast(I32),
                 in_=wc_scales[0, 4 * q : 4 * q + 4, :].bitcast(I32),
             )
+        tab1 = load_table(1)
+        wg_raw0 = load_weight(wg, 0, "wg_raw0")
+        wa_raw1 = load_weight(wa, 1, "wa_raw1")
+        wg_raw1 = load_weight(wg, 1, "wg_raw1")
         nc.sync.dma_start(lists[2][:], offs3)
         d_sb = keep.tile([P, PACK], F32, name="d_sb")
         nc.sync.dma_start(out=d_sb[:], in_=d.rearrange("(p t) -> p t", t=PACK))
-        wgo_rows = wgo.rearrange("(m t) s -> t m s", t=PACK)
-        wgo_sb = [keep.tile([P, S], F32, name=f"wgo{t}") for t in range(PACK)]
-        for t in range(PACK):
-            nc.sync.dma_start(out=wgo_sb[t][:], in_=wgo_rows[t].unsqueeze(0).to_broadcast([4, 32, S]))
+        wgo_rows = wgo.rearrange("(m t) s -> m t s", t=PACK)
+        wgo_sb = [keep.tile([P, PACK, HALF], F32, name=f"wgo{h}") for h in range(S // HALF)]
+        for h in range(S // HALF):
+            for q in (0, 2, 1, 3):
+                nc.sync.dma_start(out=wgo_sb[h][32 * q : 32 * q + 32], in_=wgo_rows[:, :, h * HALF : (h + 1) * HALF])
 
-        pages = [keep.tile([P, T2], F32, name=f"page{t}") for t in range(PACK)]
-        for t in range(PACK):
+        pages = [keep.tile([P, T2], F32, name=f"page{t}") for t in range(2)]
+        for t in range(2):
             nc.vector.memset(pages[t][:].bitcast(I32), 0)
 
         wb_w = keep.tile([P, PASSES, PACK, P], U16, name="wb_w", align_bytes=64)
@@ -104,6 +106,8 @@ def tile_list_laser_link_slots_kernel(
             in_=wc_raw[:].rearrange("p (c i t) -> p c t i", i=4, t=PACK),
         )
 
+        for t in range(2, PACK):
+            pages.append(keep.tile([P, T2], F32, name=f"page{t}", tag=f"early{t}", align_bytes=64))
         tx_sc = keep.tile([P, S], U8, name="tx_sc", align_bytes=64)
         rx_sc = keep.tile([P, S], U8, name="rx_sc", align_bytes=64)
         nc.vector.tensor_copy(rx_sc[:], tab_sc[:].indirect(lists[1][:]))
@@ -113,17 +117,22 @@ def tile_list_laser_link_slots_kernel(
                 out=rx_sc_last[32 * q : 32 * q + 4, :].bitcast(I32),
                 in_=rx_sc[32 * q + 4 : 32 * q + 8, :].bitcast(I32),
             )
+        for t in range(2, PACK):
+            nc.gpsimd.memset(pages[t][:].bitcast(I32), 0)
         w_sc = keep.tile([P, PASSES + 1, PACK, P], U8, name="w_sc", align_bytes=64)
         dealt = w_sc_raw[:].rearrange("p a (m t) -> p a t m", t=PACK)
         nc.vector.tensor_copy(out=w_sc[:, 0:PASSES], in_=dealt[:, 0:PASSES])
         nc.vector.tensor_copy(out=w_sc[:, PASSES], in_=dealt[:, PASSES])
 
-        def quantize_weight(halves, name):
-            grouped = ring.tile([P, PACK, P, PACK], BF16, name="grouped", align_bytes=64)
+        def quantize_weight(halves, name, share_with_vector=False):
+            grouped = ring.tile([P, PACK, P, PACK], BF16, name="grouped", align_bytes=64, bufs=4)
             for h, raw in enumerate(halves):
                 dst = grouped[:, :, h * P // 2 : (h + 1) * P // 2, :].rearrange("p t m j -> p m t j")
                 src = raw[:].rearrange("p j (m t) -> p m t j", t=PACK)
-                nc.scalar.activation(out=dst, in_=src, func=ACT.Copy)
+                if share_with_vector and h == 1:
+                    nc.vector.tensor_copy(out=dst, in_=src)
+                else:
+                    nc.scalar.activation(out=dst, in_=src, func=ACT.Copy)
             codes = keep.tile([P, H], U32, name=name + "_codes", align_bytes=64)
             plane = keep.tile([P, H], U8, name=name + "_plane", align_bytes=64)
             nc.vector.quantize_mx(
@@ -141,12 +150,12 @@ def tile_list_laser_link_slots_kernel(
                     picked[i, h] = g
             return picked
 
-        wa_q = [quantize_weight(wa_raw0, "wa0")]
         picked0 = gather_words(tab0, 0)
-        wg_q = [quantize_weight(wg_raw0, "wg0")]
+        wa_q = [quantize_weight(wa_raw0, "wa0")]
         picked1 = gather_words(tab1, 1)
-        wa_q.append(quantize_weight(wa_raw1, "wa1"))
-        wg_q.append(quantize_weight(wg_raw1, "wg1"))
+        wg_q = [quantize_weight(wg_raw0, "wg0")]
+        wa_q.append(quantize_weight(wa_raw1, "wa1", share_with_vector=True))
+        wg_q.append(quantize_weight(wg_raw1, "wg1", share_with_vector=True))
         picked = [picked0, picked1]
 
         banks = [psum.tile([P, 2, CHUNK], F32, name=f"bank{b}") for b in range(8)]
@@ -246,7 +255,7 @@ def tile_list_laser_link_slots_kernel(
             nc.vector.tensor_tensor(
                 pages[t][:].indirect(lists[2][:, lo // LANES : hi // LANES]),
                 y[:, t, lo:hi],
-                wgo_sb[t][:, lo:hi],
+                wgo_sb[lo // HALF][:, t, lo % HALF : lo % HALF + hi - lo],
                 ALU.mult,
             )
 

@@ -35,7 +35,7 @@ def tile_list_laser_link_slots_kernel(
         psum = ctx.enter_context(tc.psum_pool(name="psum", bufs=1))
 
         lists = [keep.tile([P, S // LANES], U16, name=f"list{i}") for i in range(3)]
-        tab_sc = keep.tile([P, T], U8, name="tab_sc", align_bytes=64)
+        tab_sc = keep.tile([P, T], U8, name="tab_sc", tag="early3", align_bytes=64)
         w_sc_raw = keep.tile([P, PASSES + 1, H], U8, name="w_sc_raw", align_bytes=64)
         rx_sc_last = keep.tile([P, S], U8, name="rx_sc_last", align_bytes=64)
         nc.gpsimd.memset(tab_sc[:, : T // 2].bitcast(I32), 0)
@@ -48,12 +48,9 @@ def tile_list_laser_link_slots_kernel(
 
         def load_weight(w, a, name):
             rows = w[a * HALF : (a + 1) * HALF, :].rearrange("(p j) c -> p j c", j=PACK)
-            halves = []
-            for h in range(2):
-                raw = keep.tile([P, PACK, H // 2], F32, name=f"{name}_{h}")
-                nc.sync.dma_start(out=raw[:], in_=rows[:, :, h * H // 2 : (h + 1) * H // 2])
-                halves.append(raw)
-            return halves
+            raw = keep.tile([P, PACK, H], F32, name=name)
+            nc.sync.dma_start(out=raw[:], in_=rows)
+            return raw
 
         def load_table(a):
             words = keep.tile([P, T], U32, name=f"tab{a}", align_bytes=64)
@@ -62,13 +59,12 @@ def tile_list_laser_link_slots_kernel(
 
         wb_raw = keep.tile([P, PASSES, 2 * H], U8, name="wb_raw", tag="early2", align_bytes=64)
         nc.sync.dma_start(out=wb_raw[:].bitcast(I32), in_=wb_words.rearrange("a p b -> p a b").bitcast(I32))
-        wc_raw = keep.tile([P, H], U32, name="wc_raw", tag="early3", align_bytes=64)
-        nc.sync.dma_start(out=wc_raw[:].bitcast(I32), in_=wc_words[0].rearrange("p c i -> p (c i)").bitcast(I32))
         for q in range(4):
-            nc.sync.dma_start(
-                out=tab_sc[32 * q : 32 * q + 4 * PASSES, :].bitcast(I32),
-                in_=tab_scales[:, 4 * q : 4 * q + 4, :].bitcast(I32),
-            )
+            for a in range(PASSES):
+                nc.sync.dma_start(
+                    out=tab_sc[32 * q + 4 * a : 32 * q + 4 * a + 4, :].bitcast(I32),
+                    in_=tab_scales[a, 4 * q : 4 * q + 4, :].bitcast(I32),
+                )
         tab0 = load_table(0)
         for q in range(4):
             nc.sync.dma_start(
@@ -76,15 +72,17 @@ def tile_list_laser_link_slots_kernel(
                 in_=wb_scales[:, 4 * q : 4 * q + 4, :].rearrange("a r c -> r a c").bitcast(I32),
             )
         wa_raw0 = load_weight(wa, 0, "wa_raw0")
+        tab1 = load_table(1)
+        wg_raw0 = load_weight(wg, 0, "wg_raw0")
+        wa_raw1 = load_weight(wa, 1, "wa_raw1")
+        wg_raw1 = load_weight(wg, 1, "wg_raw1")
+        wc_raw = keep.tile([P, H], U32, name="wc_raw", align_bytes=64)
+        nc.sync.dma_start(out=wc_raw[:].bitcast(I32), in_=wc_words[0].rearrange("p c i -> p (c i)").bitcast(I32))
         for q in range(4):
             nc.sync.dma_start(
                 out=w_sc_raw[32 * q : 32 * q + 4, PASSES, :].bitcast(I32),
                 in_=wc_scales[0, 4 * q : 4 * q + 4, :].bitcast(I32),
             )
-        tab1 = load_table(1)
-        wg_raw0 = load_weight(wg, 0, "wg_raw0")
-        wa_raw1 = load_weight(wa, 1, "wa_raw1")
-        wg_raw1 = load_weight(wg, 1, "wg_raw1")
         nc.sync.dma_start(lists[2][:], offs3)
         d_sb = keep.tile([P, PACK], F32, name="d_sb")
         nc.sync.dma_start(out=d_sb[:], in_=d.rearrange("(p t) -> p t", t=PACK))
@@ -100,14 +98,7 @@ def tile_list_laser_link_slots_kernel(
 
         wb_w = keep.tile([P, PASSES, PACK, P], U16, name="wb_w", align_bytes=64)
         nc.vector.tensor_copy(out=wb_w[:], in_=wb_raw[:].bitcast(U16).rearrange("p a (m t) -> p a t m", t=PACK))
-        wc_w = keep.tile([P, PACK, P], U32, name="wc_w", align_bytes=64)
-        nc.vector.tensor_copy(
-            out=wc_w[:].rearrange("p t (c i) -> p c t i", i=4),
-            in_=wc_raw[:].rearrange("p (c i t) -> p c t i", i=4, t=PACK),
-        )
 
-        for t in range(2, PACK):
-            pages.append(keep.tile([P, T2], F32, name=f"page{t}", tag=f"early{t}", align_bytes=64))
         tx_sc = keep.tile([P, S], U8, name="tx_sc", align_bytes=64)
         rx_sc = keep.tile([P, S], U8, name="rx_sc", align_bytes=64)
         nc.vector.tensor_copy(rx_sc[:], tab_sc[:].indirect(lists[1][:]))
@@ -118,17 +109,18 @@ def tile_list_laser_link_slots_kernel(
                 in_=rx_sc[32 * q + 4 : 32 * q + 8, :].bitcast(I32),
             )
         for t in range(2, PACK):
+            pages.append(keep.tile([P, T2], F32, name=f"page{t}", tag=f"early{t}", align_bytes=64))
+        for t in range(2, PACK):
             nc.gpsimd.memset(pages[t][:].bitcast(I32), 0)
         w_sc = keep.tile([P, PASSES + 1, PACK, P], U8, name="w_sc", align_bytes=64)
         dealt = w_sc_raw[:].rearrange("p a (m t) -> p a t m", t=PACK)
         nc.vector.tensor_copy(out=w_sc[:, 0:PASSES], in_=dealt[:, 0:PASSES])
-        nc.vector.tensor_copy(out=w_sc[:, PASSES], in_=dealt[:, PASSES])
 
-        def quantize_weight(halves, name, share_with_vector=False):
+        def quantize_weight(raw, name, share_with_vector=False):
             grouped = ring.tile([P, PACK, P, PACK], BF16, name="grouped", align_bytes=64, bufs=4)
-            for h, raw in enumerate(halves):
+            for h in range(2):
                 dst = grouped[:, :, h * P // 2 : (h + 1) * P // 2, :].rearrange("p t m j -> p m t j")
-                src = raw[:].rearrange("p j (m t) -> p m t j", t=PACK)
+                src = raw[:, :, h * H // 2 : (h + 1) * H // 2].rearrange("p j (m t) -> p m t j", t=PACK)
                 if share_with_vector and h == 1:
                     nc.vector.tensor_copy(out=dst, in_=src)
                 else:
@@ -157,12 +149,17 @@ def tile_list_laser_link_slots_kernel(
         wa_q.append(quantize_weight(wa_raw1, "wa1", share_with_vector=True))
         wg_q.append(quantize_weight(wg_raw1, "wg1", share_with_vector=True))
         picked = [picked0, picked1]
+        wc_w = keep.tile([P, PACK, P], U32, name="wc_w", align_bytes=64)
+        nc.vector.tensor_copy(
+            out=wc_w[:].rearrange("p t (c i) -> p c t i", i=4),
+            in_=wc_raw[:].rearrange("p (c i t) -> p c t i", i=4, t=PACK),
+        )
+        nc.vector.tensor_copy(out=w_sc[:, PASSES], in_=dealt[:, PASSES])
 
         banks = [psum.tile([P, 2, CHUNK], F32, name=f"bank{b}") for b in range(8)]
         pair_a = [0, 2, 1, 0]
         pair_g = [1, 3, 2, 1]
         pair_m = [0, 3, 2, 3]
-        y = keep.tile([P, PACK, S], F32, name="y")
 
         def moving(i, a, c):
             h, o = divmod(c * CHUNK, HALF)
@@ -171,7 +168,7 @@ def tile_list_laser_link_slots_kernel(
         def stage1(c):
             cols = slice(c * CHUNK, (c + 1) * CHUNK)
             x = ring.tile([P, PACK, CHUNK], F32, name="x", bufs=3)
-            size = ring.tile([P, PACK, CHUNK], F32, name="size")
+            size = [keep.tile([P, 2, CHUNK], F32, name=f"size{c}{b}", tag=f"size{c}{b}") for b in range(2)]
             for b in range(2):
                 bank = banks[2 * pair_a[c] + b]
                 for a in range(PASSES):
@@ -196,7 +193,7 @@ def tile_list_laser_link_slots_kernel(
                             start=False,
                             stop=(a == PASSES - 1 and u == 1),
                         )
-                nc.scalar.activation(out=size[:, 2 * b : 2 * b + 2, :], in_=bank[:], func=ACT.Abs)
+                nc.scalar.activation(out=size[b][:], in_=bank[:], func=ACT.Abs)
             for b in range(2):
                 bank = banks[2 * pair_g[c] + b]
                 for a in range(PASSES):
@@ -213,8 +210,11 @@ def tile_list_laser_link_slots_kernel(
                             stop=(a == PASSES - 1 and u == 1),
                         )
                 nc.vector.tensor_tensor(
-                    out=x[:, 2 * b : 2 * b + 2, :], in0=bank[:], in1=size[:, 2 * b : 2 * b + 2, :], op=ALU.max
+                    out=x[:, 2 * b : 2 * b + 2, :], in0=bank[:], in1=size[b][:], op=ALU.max
                 )
+            return x
+
+        def quantize_x(x):
             x_bf = ring.tile([P, CHUNK, PACK], BF16, name="x_bf", align_bytes=64)
             nc.scalar.copy(
                 out=x_bf[:].rearrange("p (c i) t -> p c t i", i=4),
@@ -225,10 +225,10 @@ def tile_list_laser_link_slots_kernel(
             nc.vector.quantize_mx(
                 out=codes[:].bitcast(FP8X4), scales=plane[:], in_=x_bf[:].rearrange("p c t -> p (c t)")
             )
-            return x, codes, plane
+            return codes, plane
 
         def stage2(c, x, codes, plane):
-            cols = slice(c * CHUNK, (c + 1) * CHUNK)
+            sums = []
             for b in range(2):
                 bank = banks[2 * pair_m[c] + b]
                 for u in range(2):
@@ -242,35 +242,63 @@ def tile_list_laser_link_slots_kernel(
                         start=True,
                         stop=True,
                     )
-                z = ring.tile([P, 2, CHUNK], F32, name="z", bufs=3)
+                z = ring.tile([P, 2, CHUNK], F32, name="z", bufs=6)
                 for u in range(2):
                     t = 2 * b + u
                     nc.vector.scalar_tensor_tensor(
                         out=z[:, u, :], in0=x[:, t, :], scalar=d_sb[:, t : t + 1], in1=bank[:, u, :],
                         op0=ALU.mult, op1=ALU.add,
                     )
-                nc.scalar.activation(out=y[:, 2 * b : 2 * b + 2, cols], in_=z[:], func=ACT.Tanh)
+                sums.append(z)
+            return sums
 
-        def scatter(t, lo, hi):
+        def scatter(t, lo, hi, values):
             nc.vector.tensor_tensor(
                 pages[t][:].indirect(lists[2][:, lo // LANES : hi // LANES]),
-                y[:, t, lo:hi],
+                values,
                 wgo_sb[lo // HALF][:, t, lo % HALF : lo % HALF + hi - lo],
                 ALU.mult,
             )
 
-        made0 = stage1(0)
-        made1 = stage1(1)
-        stage2(0, *made0)
-        stage2(1, *made1)
-        made2 = stage1(2)
-        made3 = stage1(3)
-        stage2(2, *made2)
-        stage2(3, *made3)
+        def y_tile(name, width, tag):
+            return keep.tile([P, 2, width], F32, name=name, tag=tag)
+
+        def tanh(dst, z):
+            nc.scalar.activation(out=dst, in_=z[:], func=ACT.Tanh)
+
+        x0 = stage1(0)
+        q0 = quantize_x(x0)
+        x1 = stage1(1)
+        q1 = quantize_x(x1)
+        z0 = stage2(0, x0, *q0)
+        y0 = [y_tile("y00", CHUNK, "y00")]
+        tanh(y0[0][:], z0[0])
+        z1 = stage2(1, x1, *q1)
+        x2 = stage1(2)
+        y0.append(y_tile("y01", CHUNK, "size20"))
+        tanh(y0[1][:], z0[1])
+        q2 = quantize_x(x2)
+        y1 = [y_tile("y10", CHUNK, "size21")]
+        tanh(y1[0][:], z1[0])
+        z2 = stage2(2, x2, *q2)
+        x3 = stage1(3)
+        y1.append(y_tile("y11", CHUNK, "size30"))
+        tanh(y1[1][:], z1[1])
+        q3 = quantize_x(x3)
+        y23 = [y_tile("y20", HALF, "size31"), y_tile("y21", HALF, "y21")]
+        tanh(y23[0][:, :, :CHUNK], z2[0])
+        z3 = stage2(3, x3, *q3)
+        tanh(y23[0][:, :, CHUNK:], z3[0])
+        tanh(y23[1][:, :, :CHUNK], z2[1])
+        tanh(y23[1][:, :, CHUNK:], z3[1])
+
         out_rows = out.rearrange("(p t) s -> t p s", t=PACK)
-        for c in range(2):
+        for c, y in enumerate((y0, y1)):
             for t in range(PACK):
-                scatter(t, c * CHUNK, (c + 1) * CHUNK)
-        for t in range(PACK):
-            scatter(t, HALF, S)
+                scatter(t, c * CHUNK, (c + 1) * CHUNK, y[t // 2][:, t % 2, :])
+        scatter(0, HALF, HALF + CHUNK, y23[0][:, 0, :CHUNK])
+        scatter(0, HALF + CHUNK, S, y23[0][:, 0, CHUNK:])
+        nc.sync.dma_start(out=out_rows[0], in_=pages[0][:])
+        for t in range(1, PACK):
+            scatter(t, HALF, S, y23[t // 2][:, t % 2, :])
             nc.sync.dma_start(out=out_rows[t], in_=pages[t][:])

@@ -18,11 +18,14 @@ ALU = mybir.AluOpType
 
 P = 128
 PACK = 4
-PASSES = K // (P * PACK)
+QUADS = 4
+K_PASS = P * PACK
+PASSES = K // K_PASS
 CHUNK = 256
-CHUNKS = S // CHUNK
-HALF = 512
+HALF = S // 2
+SCALAR_SHARE = 48
 LANES = 16
+TX, RX, SLOT = 0, 1, 2
 
 
 def tile_list_laser_link_slots_kernel(
@@ -31,263 +34,249 @@ def tile_list_laser_link_slots_kernel(
     nc = tc.nc
     with ExitStack() as ctx:
         keep = ctx.enter_context(tc.tile_pool(name="keep", bufs=1))
-        ring = ctx.enter_context(tc.tile_pool(name="ring", bufs=2))
         psum = ctx.enter_context(tc.psum_pool(name="psum", bufs=1))
 
-        lists = [keep.tile([P, S // LANES], U16, name=f"list{i}") for i in range(3)]
-        tab_sc = keep.tile([P, T], U8, name="tab_sc", tag="early3", align_bytes=64)
-        w_sc_raw = keep.tile([P, PASSES + 1, H], U8, name="w_sc_raw", align_bytes=64)
-        rx_sc_last = keep.tile([P, S], U8, name="rx_sc_last", align_bytes=64)
+        def tile(shape, dtype, name, bytes_of=None):
+            return keep.tile(shape, dtype, name=name, tag=bytes_of or name, align_bytes=64)
+
+        lists = [keep.tile([P, S // LANES], U16, name=f"list{i}") for i in (TX, RX, SLOT)]
+
+        tab_sc = tile([P, T], U8, "tab_sc")
+        w_sc_raw = tile([P, PASSES + 1, H], U8, "w_sc_raw")
+        rx_sc_last = tile([P, S], U8, "rx_sc_last")
         nc.gpsimd.memset(tab_sc[:, : T // 2].bitcast(I32), 0)
         nc.vector.memset(tab_sc[:, T // 2 :].bitcast(I32), 0)
         nc.vector.memset(w_sc_raw[:].rearrange("p a c -> p (a c)").bitcast(I32), 0)
         nc.vector.memset(rx_sc_last[:].bitcast(I32), 0)
 
-        nc.sync.dma_start(lists[0][:], offs)
-        nc.sync.dma_start(lists[1][:], offs2)
-
         def load_weight(w, a, name):
-            rows = w[a * HALF : (a + 1) * HALF, :].rearrange("(p j) c -> p j c", j=PACK)
-            raw = keep.tile([P, PACK, H], F32, name=name)
-            nc.sync.dma_start(out=raw[:], in_=rows)
+            raw = tile([P, PACK, H], F32, name)
+            rows = w[a * K_PASS : (a + 1) * K_PASS, :]
+            nc.sync.dma_start(out=raw[:], in_=rows.rearrange("(p i) c -> p i c", i=PACK))
             return raw
 
         def load_table(a):
-            words = keep.tile([P, T], U32, name=f"tab{a}", align_bytes=64)
+            words = tile([P, T], U32, f"tab{a}")
             nc.sync.dma_start(out=words[:].bitcast(I32), in_=tab_words[a].rearrange("p t i -> p (t i)").bitcast(I32))
             return words
 
-        wb_raw = keep.tile([P, PASSES, 2 * H], U8, name="wb_raw", tag="early2", align_bytes=64)
+        nc.sync.dma_start(lists[TX][:], offs)
+        nc.sync.dma_start(lists[RX][:], offs2)
+        wb_raw = tile([P, PASSES, 2 * H], U8, "wb_raw")
         nc.sync.dma_start(out=wb_raw[:].bitcast(I32), in_=wb_words.rearrange("a p b -> p a b").bitcast(I32))
-        for q in range(4):
+        for q in range(QUADS):
             for a in range(PASSES):
                 nc.sync.dma_start(
                     out=tab_sc[32 * q + 4 * a : 32 * q + 4 * a + 4, :].bitcast(I32),
                     in_=tab_scales[a, 4 * q : 4 * q + 4, :].bitcast(I32),
                 )
         tab0 = load_table(0)
-        for q in range(4):
+        for q in range(QUADS):
             nc.sync.dma_start(
                 out=w_sc_raw[32 * q : 32 * q + 4, 0:PASSES, :].bitcast(I32),
                 in_=wb_scales[:, 4 * q : 4 * q + 4, :].rearrange("a r c -> r a c").bitcast(I32),
             )
         wa_raw0 = load_weight(wa, 0, "wa_raw0")
         tab1 = load_table(1)
-        wg_raw0 = load_weight(wg, 0, "wg_raw0")
         wa_raw1 = load_weight(wa, 1, "wa_raw1")
+        wg_raw0 = load_weight(wg, 0, "wg_raw0")
         wg_raw1 = load_weight(wg, 1, "wg_raw1")
-        wc_raw = keep.tile([P, H], U32, name="wc_raw", align_bytes=64)
+        wc_raw = tile([P, H], U32, "wc_raw")
         nc.sync.dma_start(out=wc_raw[:].bitcast(I32), in_=wc_words[0].rearrange("p c i -> p (c i)").bitcast(I32))
-        for q in range(4):
+        for q in range(QUADS):
             nc.sync.dma_start(
                 out=w_sc_raw[32 * q : 32 * q + 4, PASSES, :].bitcast(I32),
                 in_=wc_scales[0, 4 * q : 4 * q + 4, :].bitcast(I32),
             )
-        nc.sync.dma_start(lists[2][:], offs3)
-        d_sb = keep.tile([P, PACK], F32, name="d_sb")
+        nc.sync.dma_start(lists[SLOT][:], offs3)
+        d_sb = tile([P, PACK], F32, "d_sb")
         nc.sync.dma_start(out=d_sb[:], in_=d.rearrange("(p t) -> p t", t=PACK))
         wgo_rows = wgo.rearrange("(m t) s -> m t s", t=PACK)
-        wgo_sb = [keep.tile([P, PACK, HALF], F32, name=f"wgo{h}") for h in range(S // HALF)]
+        wgo_sb = [tile([P, PACK, HALF], F32, f"wgo{h}") for h in range(S // HALF)]
         for h in range(S // HALF):
             for q in (0, 2, 1, 3):
                 nc.sync.dma_start(out=wgo_sb[h][32 * q : 32 * q + 32], in_=wgo_rows[:, :, h * HALF : (h + 1) * HALF])
 
-        pages = [keep.tile([P, T2], F32, name=f"page{t}") for t in range(2)]
-        for t in range(2):
-            nc.vector.memset(pages[t][:].bitcast(I32), 0)
+        def picked(dtype, name, window, which, lo, hi):
+            got = tile([P, hi - lo], dtype, name)
+            nc.vector.tensor_copy(got[:], window[:].indirect(lists[which][:, lo // LANES : hi // LANES]))
+            return got
 
-        wb_w = keep.tile([P, PASSES, PACK, P], U16, name="wb_w", align_bytes=64)
+        wb_w = tile([P, PASSES, PACK, P], U16, "wb_w")
         nc.vector.tensor_copy(out=wb_w[:], in_=wb_raw[:].bitcast(U16).rearrange("p a (m t) -> p a t m", t=PACK))
 
-        tx_sc = keep.tile([P, S], U8, name="tx_sc", align_bytes=64)
-        rx_sc = keep.tile([P, S], U8, name="rx_sc", align_bytes=64)
-        nc.vector.tensor_copy(rx_sc[:], tab_sc[:].indirect(lists[1][:]))
-        nc.vector.tensor_copy(tx_sc[:], tab_sc[:].indirect(lists[0][:]))
-        for q in range(4):
+        rx_sc = picked(U8, "rx_sc", tab_sc, RX, 0, S)
+        tx_sc = picked(U8, "tx_sc", tab_sc, TX, 0, S)
+        for q in range(QUADS):
             nc.gpsimd.dma_start(
                 out=rx_sc_last[32 * q : 32 * q + 4, :].bitcast(I32),
                 in_=rx_sc[32 * q + 4 : 32 * q + 8, :].bitcast(I32),
             )
-        for t in range(2, PACK):
-            pages.append(keep.tile([P, T2], F32, name=f"page{t}", tag=f"early{t}", align_bytes=64))
-        for t in range(2, PACK):
-            nc.gpsimd.memset(pages[t][:].bitcast(I32), 0)
-        w_sc = keep.tile([P, PASSES + 1, PACK, P], U8, name="w_sc", align_bytes=64)
-        dealt = w_sc_raw[:].rearrange("p a (m t) -> p a t m", t=PACK)
-        nc.vector.tensor_copy(out=w_sc[:, 0:PASSES], in_=dealt[:, 0:PASSES])
+        pages = [tile([P, T2], F32, f"page{t}") for t in range(PACK - 1)]
+        for page in pages:
+            nc.vector.memset(page[:].bitcast(I32), 0)
+        pages.append(tile([P, T2], F32, "page_last", "wb_raw"))
+        nc.gpsimd.memset(pages[-1][:].bitcast(I32), 0)
+        w_sc = tile([P, PASSES + 1, PACK, P], U8, "w_sc")
+        w_sc_dealt = w_sc_raw[:].rearrange("p a (m t) -> p a t m", t=PACK)
+        nc.vector.tensor_copy(out=w_sc[:, 0:PASSES], in_=w_sc_dealt[:, 0:PASSES])
 
-        def quantize_weight(raw, name, share_with_vector=False):
-            grouped = ring.tile([P, PACK, P, PACK], BF16, name="grouped", align_bytes=64, bufs=4)
-            for h in range(2):
-                dst = grouped[:, :, h * P // 2 : (h + 1) * P // 2, :].rearrange("p t m j -> p m t j")
-                src = raw[:, :, h * H // 2 : (h + 1) * H // 2].rearrange("p j (m t) -> p m t j", t=PACK)
-                if share_with_vector and h == 1:
-                    nc.vector.tensor_copy(out=dst, in_=src)
-                else:
-                    nc.scalar.activation(out=dst, in_=src, func=ACT.Copy)
-            codes = keep.tile([P, H], U32, name=name + "_codes", align_bytes=64)
-            plane = keep.tile([P, H], U8, name=name + "_plane", align_bytes=64)
-            nc.vector.quantize_mx(
-                out=codes[:].bitcast(FP8X4), scales=plane[:], in_=grouped[:].rearrange("p t m j -> p (t m j)")
-            )
-            return codes, plane
+        def quantize(grouped, name):
+            columns = grouped.shape[1] // PACK
+            words = tile([P, columns], U32, name + "_words")
+            plane = tile([P, columns], U8, name + "_plane")
+            nc.vector.quantize_mx(out=words[:].bitcast(FP8X4), scales=plane[:], in_=grouped)
+            return words, plane
 
-        def gather_words(words, a):
-            picked = {}
+        def quantize_weight(raw, name, on_scalar):
+            grouped = tile([P, PACK, P, PACK], BF16, name + "_bf")
+            dst = grouped[:].rearrange("p t m i -> p m t i")
+            src = raw[:].rearrange("p i (m t) -> p m t i", t=PACK)
+            nc.scalar.activation(out=dst[:, :on_scalar], in_=src[:, :on_scalar], func=ACT.Copy)
+            if on_scalar < P:
+                nc.vector.tensor_copy(out=dst[:, on_scalar:], in_=src[:, on_scalar:])
+            return quantize(grouped[:].rearrange("p t m i -> p (t m i)"), name)
+
+        v = {}
+
+        def gather_pass(a, words):
             for h in range(S // HALF):
-                for i in range(2):
-                    g = keep.tile([P, HALF], U32, name=f"picked{a}{h}{i}", align_bytes=64)
-                    cols = slice(h * HALF // LANES, (h + 1) * HALF // LANES)
-                    nc.vector.tensor_copy(g[:], words[:].indirect(lists[i][:, cols]))
-                    picked[i, h] = g
-            return picked
+                for which in (TX, RX):
+                    v[a, which, h] = picked(U32, f"v{a}{which}{h}", words, which, h * HALF, (h + 1) * HALF)
 
-        picked0 = gather_words(tab0, 0)
-        wa_q = [quantize_weight(wa_raw0, "wa0")]
-        picked1 = gather_words(tab1, 1)
-        wg_q = [quantize_weight(wg_raw0, "wg0")]
-        wa_q.append(quantize_weight(wa_raw1, "wa1", share_with_vector=True))
-        wg_q.append(quantize_weight(wg_raw1, "wg1", share_with_vector=True))
-        picked = [picked0, picked1]
-        wc_w = keep.tile([P, PACK, P], U32, name="wc_w", align_bytes=64)
+        gather_pass(0, tab0)
+        wa_q = [quantize_weight(wa_raw0, "wa0", P)]
+        gather_pass(1, tab1)
+        wa_q.append(quantize_weight(wa_raw1, "wa1", P))
+        wg_q = [quantize_weight(wg_raw0, "wg0", SCALAR_SHARE), quantize_weight(wg_raw1, "wg1", SCALAR_SHARE)]
+        wc_w = tile([P, PACK, P], U32, "wc_w")
         nc.vector.tensor_copy(
-            out=wc_w[:].rearrange("p t (c i) -> p c t i", i=4),
-            in_=wc_raw[:].rearrange("p (c i t) -> p c t i", i=4, t=PACK),
+            out=wc_w[:].rearrange("p t (c e) -> p c t e", e=4),
+            in_=wc_raw[:].rearrange("p (c e t) -> p c t e", e=4, t=PACK),
         )
-        nc.vector.tensor_copy(out=w_sc[:, PASSES], in_=dealt[:, PASSES])
+        nc.vector.tensor_copy(out=w_sc[:, PASSES], in_=w_sc_dealt[:, PASSES])
 
         banks = [psum.tile([P, 2, CHUNK], F32, name=f"bank{b}") for b in range(8)]
-        pair_a = [0, 2, 1, 0]
-        pair_g = [1, 3, 2, 1]
-        pair_m = [0, 3, 2, 3]
+        turns = [("both", 0), ("floor", 0), ("both", 1), ("floor", 1)]
+        for c in range(S // CHUNK):
+            turns.append(("mixed", c))
+            if c + 2 < S // CHUNK:
+                turns.extend([("both", c + 2), ("floor", c + 2)])
 
-        def moving(i, a, c):
-            h, o = divmod(c * CHUNK, HALF)
-            return picked[a][i, h][:, o : o + CHUNK].bitcast(FP8X4)
+        def bank_of(kind, c, b):
+            return banks[2 * (turns.index((kind, c)) % 4) + b]
 
-        def stage1(c):
-            cols = slice(c * CHUNK, (c + 1) * CHUNK)
-            x = ring.tile([P, PACK, CHUNK], F32, name="x", bufs=3)
-            size = [keep.tile([P, 2, CHUNK], F32, name=f"size{c}{b}", tag=f"size{c}{b}") for b in range(2)]
-            for b in range(2):
-                bank = banks[2 * pair_a[c] + b]
-                for a in range(PASSES):
-                    for u in range(2):
-                        t = 2 * b + u
-                        m = slice(t * P, (t + 1) * P)
-                        nc.tensor.matmul_mx(
-                            out=bank[:, u, :],
-                            lhsT=wa_q[a][0][:, m].bitcast(FP8X4),
-                            lhsT_scale=wa_q[a][1][:, m],
-                            rhs=moving(0, a, c),
-                            rhs_scale=tx_sc[4 * a : P, cols],
-                            start=(a == 0 and u == 0),
-                            stop=False,
-                        )
-                        nc.tensor.matmul_mx(
-                            out=bank[:, u, :],
-                            lhsT=wb_w[:, a, t, :].bitcast(FP4X4),
-                            lhsT_scale=w_sc[:, a, t, :],
-                            rhs=moving(1, a, c),
-                            rhs_scale=(rx_sc if a == 0 else rx_sc_last)[:, cols],
-                            start=False,
-                            stop=(a == PASSES - 1 and u == 1),
-                        )
-                nc.scalar.activation(out=size[b][:], in_=bank[:], func=ACT.Abs)
-            for b in range(2):
-                bank = banks[2 * pair_g[c] + b]
-                for a in range(PASSES):
-                    for u in range(2):
-                        t = 2 * b + u
-                        m = slice(t * P, (t + 1) * P)
-                        nc.tensor.matmul_mx(
-                            out=bank[:, u, :],
-                            lhsT=wg_q[a][0][:, m].bitcast(FP8X4),
-                            lhsT_scale=wg_q[a][1][:, m],
-                            rhs=moving(0, a, c),
-                            rhs_scale=tx_sc[4 * a : P, cols],
-                            start=(a == 0 and u == 0),
-                            stop=(a == PASSES - 1 and u == 1),
-                        )
-                nc.vector.tensor_tensor(
-                    out=x[:, 2 * b : 2 * b + 2, :], in0=bank[:], in1=size[b][:], op=ALU.max
+        def first_stage(c, bytes_of):
+            links = slice(c * CHUNK, (c + 1) * CHUNK)
+            h, start = divmod(c * CHUNK, HALF)
+            order = [(a, u) for a in range(PASSES) for u in range(2)]
+
+            def product(bank, u, words, plane, which, a, first, last):
+                nc.tensor.matmul_mx(
+                    out=bank[:, u, :],
+                    lhsT=words,
+                    lhsT_scale=plane,
+                    rhs=v[a, which, h][:, start : start + CHUNK].bitcast(FP8X4),
+                    rhs_scale=tx_sc[4 * a : P, links] if which == TX else (rx_sc, rx_sc_last)[a][:, links],
+                    start=first,
+                    stop=last,
                 )
+
+            x = tile([P, PACK, CHUNK], F32, f"x{c}", bytes_of)
+            sizes = []
+            for b in range(2):
+                bank = bank_of("both", c, b)
+                for a, u in order:
+                    t = 2 * b + u
+                    product(bank, u, wb_w[:, a, t].bitcast(FP4X4), w_sc[:, a, t], RX, a, (a, u) == order[0], False)
+                for a, u in order:
+                    words, plane = wa_q[a]
+                    cols = slice((2 * b + u) * P, (2 * b + u + 1) * P)
+                    product(bank, u, words[:, cols].bitcast(FP8X4), plane[:, cols], TX, a, False, (a, u) == order[-1])
+                size = tile([P, 2, CHUNK], F32, f"size{c}{b}")
+                nc.scalar.activation(out=size[:], in_=bank[:], func=ACT.Abs)
+                sizes.append(size)
+            for b in range(2):
+                bank = bank_of("floor", c, b)
+                for a, u in order:
+                    words, plane = wg_q[a]
+                    cols = slice((2 * b + u) * P, (2 * b + u + 1) * P)
+                    first, last = (a, u) == order[0], (a, u) == order[-1]
+                    product(bank, u, words[:, cols].bitcast(FP8X4), plane[:, cols], TX, a, first, last)
+                nc.vector.tensor_tensor(out=x[:, 2 * b : 2 * b + 2, :], in0=bank[:], in1=sizes[b][:], op=ALU.max)
             return x
 
-        def quantize_x(x):
-            x_bf = ring.tile([P, CHUNK, PACK], BF16, name="x_bf", align_bytes=64)
+        def quantize_x(c, x):
+            grouped = tile([P, CHUNK, PACK], BF16, f"x{c}_bf")
             nc.scalar.copy(
-                out=x_bf[:].rearrange("p (c i) t -> p c t i", i=4),
-                in_=x[:].rearrange("p t (c i) -> p c t i", i=4),
+                out=grouped[:].rearrange("p (c e) t -> p c t e", e=4),
+                in_=x[:].rearrange("p t (c e) -> p c t e", e=4),
             )
-            codes = ring.tile([P, CHUNK], U32, name="x_codes", align_bytes=64)
-            plane = ring.tile([P, CHUNK], U8, name="x_plane", align_bytes=64)
-            nc.vector.quantize_mx(
-                out=codes[:].bitcast(FP8X4), scales=plane[:], in_=x_bf[:].rearrange("p c t -> p (c t)")
-            )
-            return codes, plane
+            return quantize(grouped[:].rearrange("p c t -> p (c t)"), f"x{c}")
 
-        def stage2(c, x, codes, plane):
+        def second_stage(c, x, words, plane):
             sums = []
             for b in range(2):
-                bank = banks[2 * pair_m[c] + b]
+                bank = bank_of("mixed", c, b)
                 for u in range(2):
-                    t = 2 * b + u
                     nc.tensor.matmul_mx(
                         out=bank[:, u, :],
-                        lhsT=wc_w[:, t, :].bitcast(FP8X4),
-                        lhsT_scale=w_sc[:, PASSES, t, :],
-                        rhs=codes[:].bitcast(FP8X4),
+                        lhsT=wc_w[:, 2 * b + u].bitcast(FP8X4),
+                        lhsT_scale=w_sc[:, PASSES, 2 * b + u],
+                        rhs=words[:].bitcast(FP8X4),
                         rhs_scale=plane[:],
                         start=True,
                         stop=True,
                     )
-                z = ring.tile([P, 2, CHUNK], F32, name="z", bufs=6)
+                z = tile([P, 2, CHUNK], F32, f"z{c}{b}")
                 for u in range(2):
                     t = 2 * b + u
                     nc.vector.scalar_tensor_tensor(
-                        out=z[:, u, :], in0=x[:, t, :], scalar=d_sb[:, t : t + 1], in1=bank[:, u, :],
-                        op0=ALU.mult, op1=ALU.add,
+                        out=z[:, u, :],
+                        in0=x[:, t, :],
+                        scalar=d_sb[:, t : t + 1],
+                        in1=bank[:, u, :],
+                        op0=ALU.mult,
+                        op1=ALU.add,
                     )
                 sums.append(z)
             return sums
 
-        def scatter(t, lo, hi, values):
+        def tanh(y, z):
+            nc.scalar.activation(out=y, in_=z[:], func=ACT.Tanh)
+
+        def scatter(t, lo, hi, y):
             nc.vector.tensor_tensor(
-                pages[t][:].indirect(lists[2][:, lo // LANES : hi // LANES]),
-                values,
+                pages[t][:].indirect(lists[SLOT][:, lo // LANES : hi // LANES]),
+                y,
                 wgo_sb[lo // HALF][:, t, lo % HALF : lo % HALF + hi - lo],
                 ALU.mult,
             )
 
-        def y_tile(name, width, tag):
-            return keep.tile([P, 2, width], F32, name=name, tag=tag)
-
-        def tanh(dst, z):
-            nc.scalar.activation(out=dst, in_=z[:], func=ACT.Tanh)
-
-        x0 = stage1(0)
-        q0 = quantize_x(x0)
-        x1 = stage1(1)
-        q1 = quantize_x(x1)
-        z0 = stage2(0, x0, *q0)
-        y0 = [y_tile("y00", CHUNK, "y00")]
+        x0 = first_stage(0, "wa_raw0")
+        x0_q = quantize_x(0, x0)
+        x1 = first_stage(1, "wa_raw1")
+        x1_q = quantize_x(1, x1)
+        z0 = second_stage(0, x0, *x0_q)
+        y0 = [tile([P, 2, CHUNK], F32, "y00")]
         tanh(y0[0][:], z0[0])
-        z1 = stage2(1, x1, *q1)
-        x2 = stage1(2)
-        y0.append(y_tile("y01", CHUNK, "size20"))
+        z1 = second_stage(1, x1, *x1_q)
+
+        x2 = first_stage(2, "wg_raw0")
+        y0.append(tile([P, 2, CHUNK], F32, "y01", "size20"))
         tanh(y0[1][:], z0[1])
-        q2 = quantize_x(x2)
-        y1 = [y_tile("y10", CHUNK, "size21")]
+        x2_q = quantize_x(2, x2)
+        y1 = [tile([P, 2, CHUNK], F32, "y10", "size21")]
         tanh(y1[0][:], z1[0])
-        z2 = stage2(2, x2, *q2)
-        x3 = stage1(3)
-        y1.append(y_tile("y11", CHUNK, "size30"))
+        z2 = second_stage(2, x2, *x2_q)
+
+        x3 = first_stage(3, "wg_raw1")
+        y1.append(tile([P, 2, CHUNK], F32, "y11", "size30"))
         tanh(y1[1][:], z1[1])
-        q3 = quantize_x(x3)
-        y23 = [y_tile("y20", HALF, "size31"), y_tile("y21", HALF, "y21")]
+        x3_q = quantize_x(3, x3)
+        y23 = [tile([P, 2, HALF], F32, "y230", "size31"), tile([P, 2, HALF], F32, "y231")]
         tanh(y23[0][:, :, :CHUNK], z2[0])
-        z3 = stage2(3, x3, *q3)
+        z3 = second_stage(3, x3, *x3_q)
         tanh(y23[0][:, :, CHUNK:], z3[0])
         tanh(y23[1][:, :, :CHUNK], z2[1])
         tanh(y23[1][:, :, CHUNK:], z3[1])

from contextlib import ExitStack

import concourse.mybir as mybir

K, H, T, S, T2 = 1024, 512, 4096, 1024, 2048
FLOPS = 2 * S * H * (3 * K + H)

F32 = mybir.dt.float32
BF16 = mybir.dt.bfloat16
I32 = mybir.dt.int32
U32 = mybir.dt.uint32
U16 = mybir.dt.uint16
U8 = mybir.dt.uint8
FP8X4 = mybir.dt.float8_e4m3fn_x4
FP4X4 = mybir.dt.float4_e2m1fn_x4
ACT = mybir.ActivationFunctionType
ALU = mybir.AluOpType

P = 128
PACK = 4
QUADS = 4
K_PASS = P * PACK
PASSES = K // K_PASS
CHUNK = 256
HALF = S // 2
SCALAR_SHARE = 48
LANES = 16
TX, RX, SLOT = 0, 1, 2


def tile_list_laser_link_slots_kernel(
    tc, tab_words, tab_scales, offs, offs2, offs3, wa, wb_words, wb_scales, wg, wc_words, wc_scales, d, wgo, out
):
    nc = tc.nc
    with ExitStack() as ctx:
        keep = ctx.enter_context(tc.tile_pool(name="keep", bufs=1))
        psum = ctx.enter_context(tc.psum_pool(name="psum", bufs=1))

        def tile(shape, dtype, name, bytes_of=None):
            return keep.tile(shape, dtype, name=name, tag=bytes_of or name, align_bytes=64)

        lists = [keep.tile([P, S // LANES], U16, name=f"list{i}") for i in (TX, RX, SLOT)]

        tab_sc = tile([P, T], U8, "tab_sc")
        w_sc_raw = tile([P, PASSES + 1, H], U8, "w_sc_raw")
        rx_sc_last = tile([P, S], U8, "rx_sc_last")
        nc.gpsimd.memset(tab_sc[:, : T // 2].bitcast(I32), 0)
        nc.vector.memset(tab_sc[:, T // 2 :].bitcast(I32), 0)
        nc.vector.memset(w_sc_raw[:].rearrange("p a c -> p (a c)").bitcast(I32), 0)
        nc.vector.memset(rx_sc_last[:].bitcast(I32), 0)

        def load_weight(w, a, name):
            raw = tile([P, PACK, H], F32, name)
            rows = w[a * K_PASS : (a + 1) * K_PASS, :]
            nc.sync.dma_start(out=raw[:], in_=rows.rearrange("(p i) c -> p i c", i=PACK))
            return raw

        def load_table(a):
            words = tile([P, T], U32, f"tab{a}")
            nc.sync.dma_start(out=words[:].bitcast(I32), in_=tab_words[a].rearrange("p t i -> p (t i)").bitcast(I32))
            return words

        nc.sync.dma_start(lists[TX][:], offs)
        nc.sync.dma_start(lists[RX][:], offs2)
        wb_raw = tile([P, PASSES, 2 * H], U8, "wb_raw")
        nc.sync.dma_start(out=wb_raw[:].bitcast(I32), in_=wb_words.rearrange("a p b -> p a b").bitcast(I32))
        for q in range(QUADS):
            for a in range(PASSES):
                nc.sync.dma_start(
                    out=tab_sc[32 * q + 4 * a : 32 * q + 4 * a + 4, :].bitcast(I32),
                    in_=tab_scales[a, 4 * q : 4 * q + 4, :].bitcast(I32),
                )
        tab0 = load_table(0)
        for q in range(QUADS):
            nc.sync.dma_start(
                out=w_sc_raw[32 * q : 32 * q + 4, 0:PASSES, :].bitcast(I32),
                in_=wb_scales[:, 4 * q : 4 * q + 4, :].rearrange("a r c -> r a c").bitcast(I32),
            )
        wa_raw0 = load_weight(wa, 0, "wa_raw0")
        tab1 = load_table(1)
        wa_raw1 = load_weight(wa, 1, "wa_raw1")
        wg_raw0 = load_weight(wg, 0, "wg_raw0")
        wg_raw1 = load_weight(wg, 1, "wg_raw1")
        wc_raw = tile([P, H], U32, "wc_raw")
        nc.sync.dma_start(out=wc_raw[:].bitcast(I32), in_=wc_words[0].rearrange("p c i -> p (c i)").bitcast(I32))
        for q in range(QUADS):
            nc.sync.dma_start(
                out=w_sc_raw[32 * q : 32 * q + 4, PASSES, :].bitcast(I32),
                in_=wc_scales[0, 4 * q : 4 * q + 4, :].bitcast(I32),
            )
        nc.sync.dma_start(lists[SLOT][:], offs3)
        d_sb = tile([P, PACK], F32, "d_sb")
        nc.sync.dma_start(out=d_sb[:], in_=d.rearrange("(p t) -> p t", t=PACK))
        wgo_rows = wgo.rearrange("(m t) s -> m t s", t=PACK)
        wgo_sb = [tile([P, PACK, HALF], F32, f"wgo{h}") for h in range(S // HALF)]
        for h in range(S // HALF):
            for q in (0, 2, 1, 3):
                nc.sync.dma_start(out=wgo_sb[h][32 * q : 32 * q + 32], in_=wgo_rows[:, :, h * HALF : (h + 1) * HALF])

        def picked(dtype, name, window, which, lo, hi):
            got = tile([P, hi - lo], dtype, name)
            nc.vector.tensor_copy(got[:], window[:].indirect(lists[which][:, lo // LANES : hi // LANES]))
            return got

        wb_w = tile([P, PASSES, PACK, P], U16, "wb_w")
        nc.vector.tensor_copy(out=wb_w[:], in_=wb_raw[:].bitcast(U16).rearrange("p a (m t) -> p a t m", t=PACK))

        rx_sc = picked(U8, "rx_sc", tab_sc, RX, 0, S)
        tx_sc = picked(U8, "tx_sc", tab_sc, TX, 0, S)
        for q in range(QUADS):
            nc.gpsimd.dma_start(
                out=rx_sc_last[32 * q : 32 * q + 4, :].bitcast(I32),
                in_=rx_sc[32 * q + 4 : 32 * q + 8, :].bitcast(I32),
            )
        pages = [tile([P, T2], F32, f"page{t}") for t in range(PACK - 1)]
        for page in pages:
            nc.vector.memset(page[:].bitcast(I32), 0)
        pages.append(tile([P, T2], F32, "page_last", "wb_raw"))
        nc.gpsimd.memset(pages[-1][:].bitcast(I32), 0)
        w_sc = tile([P, PASSES + 1, PACK, P], U8, "w_sc")
        w_sc_dealt = w_sc_raw[:].rearrange("p a (m t) -> p a t m", t=PACK)
        nc.vector.tensor_copy(out=w_sc[:, 0:PASSES], in_=w_sc_dealt[:, 0:PASSES])

        def quantize(grouped, name):
            columns = grouped.shape[1] // PACK
            words = tile([P, columns], U32, name + "_words")
            plane = tile([P, columns], U8, name + "_plane")
            nc.vector.quantize_mx(out=words[:].bitcast(FP8X4), scales=plane[:], in_=grouped)
            return words, plane

        def quantize_weight(raw, name, on_scalar):
            grouped = tile([P, PACK, P, PACK], BF16, name + "_bf")
            dst = grouped[:].rearrange("p t m i -> p m t i")
            src = raw[:].rearrange("p i (m t) -> p m t i", t=PACK)
            nc.scalar.activation(out=dst[:, :on_scalar], in_=src[:, :on_scalar], func=ACT.Copy)
            if on_scalar < P:
                nc.vector.tensor_copy(out=dst[:, on_scalar:], in_=src[:, on_scalar:])
            return quantize(grouped[:].rearrange("p t m i -> p (t m i)"), name)

        v = {}

        def gather_pass(a, words):
            for h in range(S // HALF):
                for which in (TX, RX):
                    v[a, which, h] = picked(U32, f"v{a}{which}{h}", words, which, h * HALF, (h + 1) * HALF)

        gather_pass(0, tab0)
        wa_q = [quantize_weight(wa_raw0, "wa0", P)]
        gather_pass(1, tab1)
        wa_q.append(quantize_weight(wa_raw1, "wa1", P))
        wg_q = [quantize_weight(wg_raw0, "wg0", SCALAR_SHARE), quantize_weight(wg_raw1, "wg1", SCALAR_SHARE)]
        wc_w = tile([P, PACK, P], U32, "wc_w")
        nc.vector.tensor_copy(
            out=wc_w[:].rearrange("p t (c e) -> p c t e", e=4),
            in_=wc_raw[:].rearrange("p (c e t) -> p c t e", e=4, t=PACK),
        )
        nc.vector.tensor_copy(out=w_sc[:, PASSES], in_=w_sc_dealt[:, PASSES])

        banks = [psum.tile([P, 2, CHUNK], F32, name=f"bank{b}") for b in range(8)]
        turns = [("both", 0), ("floor", 0), ("both", 1), ("floor", 1)]
        for c in range(S // CHUNK):
            turns.append(("mixed", c))
            if c + 2 < S // CHUNK:
                turns.extend([("both", c + 2), ("floor", c + 2)])

        def bank_of(kind, c, b):
            return banks[2 * (turns.index((kind, c)) % 4) + b]

        def first_stage(c, bytes_of):
            links = slice(c * CHUNK, (c + 1) * CHUNK)
            h, start = divmod(c * CHUNK, HALF)
            order = [(a, u) for a in range(PASSES) for u in range(2)]

            def product(bank, u, words, plane, which, a, first, last):
                nc.tensor.matmul_mx(
                    out=bank[:, u, :],
                    lhsT=words,
                    lhsT_scale=plane,
                    rhs=v[a, which, h][:, start : start + CHUNK].bitcast(FP8X4),
                    rhs_scale=tx_sc[4 * a : P, links] if which == TX else (rx_sc, rx_sc_last)[a][:, links],
                    start=first,
                    stop=last,
                )

            x = tile([P, PACK, CHUNK], F32, f"x{c}", bytes_of)
            sizes = []
            for b in range(2):
                bank = bank_of("both", c, b)
                for a, u in order:
                    t = 2 * b + u
                    product(bank, u, wb_w[:, a, t].bitcast(FP4X4), w_sc[:, a, t], RX, a, (a, u) == order[0], False)
                for a, u in order:
                    words, plane = wa_q[a]
                    cols = slice((2 * b + u) * P, (2 * b + u + 1) * P)
                    product(bank, u, words[:, cols].bitcast(FP8X4), plane[:, cols], TX, a, False, (a, u) == order[-1])
                size = tile([P, 2, CHUNK], F32, f"size{c}{b}")
                nc.scalar.activation(out=size[:], in_=bank[:], func=ACT.Abs)
                sizes.append(size)
            for b in range(2):
                bank = bank_of("floor", c, b)
                for a, u in order:
                    words, plane = wg_q[a]
                    cols = slice((2 * b + u) * P, (2 * b + u + 1) * P)
                    first, last = (a, u) == order[0], (a, u) == order[-1]
                    product(bank, u, words[:, cols].bitcast(FP8X4), plane[:, cols], TX, a, first, last)
                nc.vector.tensor_tensor(out=x[:, 2 * b : 2 * b + 2, :], in0=bank[:], in1=sizes[b][:], op=ALU.max)
            return x

        def quantize_x(c, x):
            grouped = tile([P, CHUNK, PACK], BF16, f"x{c}_bf")
            nc.scalar.copy(
                out=grouped[:].rearrange("p (c e) t -> p c t e", e=4),
                in_=x[:].rearrange("p t (c e) -> p c t e", e=4),
            )
            return quantize(grouped[:].rearrange("p c t -> p (c t)"), f"x{c}")

        def second_stage(c, x, words, plane):
            sums = []
            for b in range(2):
                bank = bank_of("mixed", c, b)
                for u in range(2):
                    nc.tensor.matmul_mx(
                        out=bank[:, u, :],
                        lhsT=wc_w[:, 2 * b + u].bitcast(FP8X4),
                        lhsT_scale=w_sc[:, PASSES, 2 * b + u],
                        rhs=words[:].bitcast(FP8X4),
                        rhs_scale=plane[:],
                        start=True,
                        stop=True,
                    )
                z = tile([P, 2, CHUNK], F32, f"z{c}{b}")
                for u in range(2):
                    t = 2 * b + u
                    nc.vector.scalar_tensor_tensor(
                        out=z[:, u, :],
                        in0=x[:, t, :],
                        scalar=d_sb[:, t : t + 1],
                        in1=bank[:, u, :],
                        op0=ALU.mult,
                        op1=ALU.add,
                    )
                sums.append(z)
            return sums

        def tanh(y, z):
            nc.scalar.activation(out=y, in_=z[:], func=ACT.Tanh)

        def scatter(t, lo, hi, y):
            nc.vector.tensor_tensor(
                pages[t][:].indirect(lists[SLOT][:, lo // LANES : hi // LANES]),
                y,
                wgo_sb[lo // HALF][:, t, lo % HALF : lo % HALF + hi - lo],
                ALU.mult,
            )

        x0 = first_stage(0, "wa_raw0")
        x0_q = quantize_x(0, x0)
        x1 = first_stage(1, "wa_raw1")
        x1_q = quantize_x(1, x1)
        z0 = second_stage(0, x0, *x0_q)
        y0 = [tile([P, 2, CHUNK], F32, "y00")]
        tanh(y0[0][:], z0[0])
        z1 = second_stage(1, x1, *x1_q)

        x2 = first_stage(2, "wg_raw0")
        y0.append(tile([P, 2, CHUNK], F32, "y01", "size20"))
        tanh(y0[1][:], z0[1])
        x2_q = quantize_x(2, x2)
        y1 = [tile([P, 2, CHUNK], F32, "y10", "size21")]
        tanh(y1[0][:], z1[0])
        z2 = second_stage(2, x2, *x2_q)

        x3 = first_stage(3, "wg_raw1")
        y1.append(tile([P, 2, CHUNK], F32, "y11", "size30"))
        tanh(y1[1][:], z1[1])
        x3_q = quantize_x(3, x3)
        y23 = [tile([P, 2, HALF], F32, "y230", "size31"), tile([P, 2, HALF], F32, "y231")]
        tanh(y23[0][:, :, :CHUNK], z2[0])
        z3 = second_stage(3, x3, *x3_q)
        tanh(y23[0][:, :, CHUNK:], z3[0])
        tanh(y23[1][:, :, :CHUNK], z2[1])
        tanh(y23[1][:, :, CHUNK:], z3[1])

        out_rows = out.rearrange("(p t) s -> t p s", t=PACK)
        for c, y in enumerate((y0, y1)):
            for t in range(PACK):
                scatter(t, c * CHUNK, (c + 1) * CHUNK, y[t // 2][:, t % 2, :])
        scatter(0, HALF, HALF + CHUNK, y23[0][:, 0, :CHUNK])
        scatter(0, HALF + CHUNK, S, y23[0][:, 0, CHUNK:])
        nc.sync.dma_start(out=out_rows[0], in_=pages[0][:])
        for t in range(1, PACK):
            scatter(t, HALF, S, y23[t // 2][:, t % 2, :])
            nc.sync.dma_start(out=out_rows[t], in_=pages[t][:])
